import numpy as np
import ml_dtypes


def mxq(x, axis, fmt="e4m3"):
    dtype, down = {"e4m3": (ml_dtypes.float8_e4m3fn, 7), "e5m2": (ml_dtypes.float8_e5m2, 14)}[fmt]
    v = np.moveaxis(np.asarray(x, np.float32).astype(ml_dtypes.bfloat16).astype(np.float64), axis, -1)
    blocks = v.reshape(v.shape[:-1] + (-1, 32))
    amax = np.abs(blocks).max(-1, keepdims=True)
    byte = np.maximum(np.where(amax > 0, np.frexp(amax)[1] - 1 + 127, 0) - down, 1)
    scale = np.exp2(byte - 127.0)
    codes = (blocks / scale).astype(np.float32).astype(dtype).astype(np.float64)
    return np.moveaxis((codes * scale).reshape(v.shape), -1, axis)


WIDE = False


def mx_kscale(k):
    if not WIDE:
        return np.ones(k)
    levels = np.array([10, -10, 5, -5, 0])
    if k % 512:
        return np.exp2(np.random.permutation(np.resize(levels, k // 32))).repeat(32)
    a = np.empty((k // 512, 16))
    for p in range(k // 512):
        a[p, :8] = np.random.permutation(np.resize(levels, 8))
        for g in range(8):
            far = levels[np.abs(levels - a[p, g]) >= 10]
            a[p, g + 8] = far[np.random.randint(len(far))]
    return np.exp2(a.ravel()).repeat(32)


BF16 = ml_dtypes.bfloat16


def bf(x):
    return np.asarray(x, np.float32).astype(BF16)


def f64(x):
    return np.asarray(x).astype(np.float64)


E2M1 = np.array([0.0, 0.5, 1.0, 1.5, 2.0, 3.0, 4.0, 6.0, -0.0, -0.5, -1.0, -1.5, -2.0, -3.0, -4.0, -6.0])


def pack_weight(w, fmt):
    k, n = w.shape
    w = f64(bf(w)).reshape(k // 32, 32, n)
    amax = np.abs(w).max(1)
    if fmt == "e4m3":
        byte = np.frexp(amax)[1] - 1 + 127 - 7
    else:
        mant, ex = np.frexp(amax / 6.0)
        byte = np.where(mant > 0.5, ex, ex - 1) + 127
    byte = np.clip(np.where(amax > 0, byte, 1), 1, 254)
    scaled = (w * np.exp2(127.0 - byte)[:, None, :]).reshape(k, n).astype(np.float32)
    by_word = np.ascontiguousarray(scaled.reshape(k // 512, 128, 4, n).transpose(0, 1, 3, 2))
    if fmt == "e4m3":
        words = by_word.astype(ml_dtypes.float8_e4m3fn).view(np.uint8)
    else:
        c = by_word.astype(ml_dtypes.float4_e2m1fn).view(np.uint8) & 0xF
        words = c[..., 0::2] | (c[..., 1::2] << 4)
    return np.ascontiguousarray(words), np.ascontiguousarray(byte.astype(np.uint8).reshape(k // 512, 16, n))


def unpack_weight(words, scales, fmt):
    g, p, n, _ = words.shape
    if fmt == "e4m3":
        vals = np.ascontiguousarray(words).view(ml_dtypes.float8_e4m3fn).astype(np.float64)
    else:
        nib = np.empty((g, p, n, 4), np.uint8)
        nib[..., 0::2] = words & 0xF
        nib[..., 1::2] = words >> 4
        vals = E2M1[nib]
    vals = vals * np.repeat(np.exp2(scales.astype(np.float64) - 127.0), 8, axis=1)[..., None]
    return vals.transpose(0, 1, 3, 2).reshape(g * 512, n)

def planes(Y):
    n, m = Y.shape
    b = f64(bf(Y)).reshape(n // 32, 32, m)
    amax = np.abs(b).max(1)
    byte = np.clip(np.where(amax > 0, np.frexp(amax)[1] - 1 + 127 - 7, 1), 1, 254)
    codes = (b * np.exp2(127.0 - byte)[:, None, :]).reshape(n, m).astype(np.float32).astype(ml_dtypes.float8_e4m3fn).view(np.uint8)
    words = codes.reshape(n // 512, 128, 4, m).transpose(0, 1, 3, 2)
    return np.ascontiguousarray(words), np.ascontiguousarray(byte.astype(np.uint8).reshape(n // 512, 16, m))


B, N, E, K, D = 4, 1024, 1024, 256, 1024

EPS = 1e-5


def softmax_last(v):
    e = np.exp(v - np.max(v, axis=-1, keepdims=True))
    return e / np.sum(e, axis=-1, keepdims=True)


def soft_assign(y, w, b):
    logits = (mxq(y, 2, "e4m3") @ w) + b
    return softmax_last(logits)


def rms_intra_norm(v):
    mean_sq = np.mean(v * v, axis=-1, keepdims=True)
    return v / np.sqrt(mean_sq + EPS)


def setup_inputs():
    s, u = mx_kscale(E), mx_kscale(N)
    y = bf(np.random.standard_normal((B, N, E)) * s)
    words, scales = pack_weight(np.random.standard_normal((E, K)) * (1.5 / np.sqrt(E)) / s[:, None], "e4m3")
    return {"y": y,
            "w_words": words,
            "w_scales": scales,
            "b": bf(np.random.standard_normal(K) * 0.5),
            "t": bf(np.random.standard_normal(N) * 0.25 * u),
            "x": bf(np.random.standard_normal((B, N, D)) * (0.016 * K / np.sqrt(N)) / u[:, None]),
            "c": bf(np.random.standard_normal((K, D)) * (0.012 * K / N))}


def core(y, w_words, w_scales, b, t, x, c):
    a = soft_assign(f64(y), unpack_weight(w_words, w_scales, "e4m3"), f64(b))
    r = a * f64(t)[None, :, None]
    rq = mxq(r, 1, "e4m3")
    xq = mxq(f64(x), 1, "e4m3")
    sums = rq.transpose(0, 2, 1) @ xq
    m = np.sum(a, axis=1)
    v = sums - m[:, :, None] * f64(c)[None, :, :]
    return rms_intra_norm(v)


def reference(y, w_words, w_scales, b, t, x, c):
    R_out = core(y, w_words, w_scales, b, t, x, c)
    words, scales = planes(np.moveaxis(R_out, 2, 0).reshape(1024, -1))
    return R_out, words, scales

from contextlib import ExitStack

import concourse.mybir as mybir
from concourse.masks import make_identity

B, N, E, K, D = 4, 1024, 1024, 256, 1024
FLOPS = 2 * B * N * E * K + 2 * B * N * K * D

F32 = mybir.dt.float32
BF16 = mybir.dt.bfloat16
U32 = mybir.dt.uint32
I32 = mybir.dt.int32
U8 = mybir.dt.uint8
FP8X4 = mybir.dt.float8_e4m3fn_x4
ALU = mybir.AluOpType
ACT = mybir.ActivationFunctionType
AX = mybir.AxisListType

P = 128
XV = 448
EPS = 1e-5
HALVES = 2 * B


def tile_crossmodalreweightedvlad_x2_kernel(tc, y, w_words, w_scales, b, t, x, c, out_0, out_1, out_2):
    nc = tc.nc
    with ExitStack() as ctx:
        const = ctx.enter_context(tc.tile_pool(name="const", bufs=1))
        ypool = ctx.enter_context(tc.tile_pool(name="ypool", bufs=4))
        xpool = ctx.enter_context(tc.tile_pool(name="xpool", bufs=4))
        work = ctx.enter_context(tc.tile_pool(name="work", bufs=2))
        four = ctx.enter_context(tc.tile_pool(name="four", bufs=4))
        six = ctx.enter_context(tc.tile_pool(name="six", bufs=6))
        three = ctx.enter_context(tc.tile_pool(name="three", bufs=3))
        yt_ps = ctx.enter_context(tc.psum_pool(name="yt_ps", bufs=3))
        lg_ps = ctx.enter_context(tc.psum_pool(name="lg_ps", bufs=2))
        s_ps = ctx.enter_context(tc.psum_pool(name="s_ps", bufs=2))
        m_ps = ctx.enter_context(tc.psum_pool(name="m_ps", bufs=1))
        ctx.enter_context(tc.manual_schedule())

        ident = const.tile([P, P], F32, name="ident")
        warm = const.tile([P, 1], F32, name="warm")
        wsc = const.tile([P, 2 * K], U8, align_bytes=64, name="wsc")
        brow = const.tile([P, K], BF16, name="brow")
        ones = const.tile([P, P], BF16, name="ones")
        neghalf = const.tile([P, 1], F32, name="neghalf")
        wt = const.tile([P, 2, K], U32, align_bytes=64, name="wt")
        tb = const.tile([P, 2, 4], BF16, name="tb")
        cb = const.tile([P, 2, D], BF16, name="cb")
        cneg = const.tile([P, 2, D], BF16, name="cneg")
        bias = const.tile([P, 2, K], F32, name="bias")
        sq = const.tile([P, D], BF16, name="sq")

        yraws, xraws = {}, {}

        def load_y(j, pieces=1):
            i, h = divmod(j, 2)
            yraw = ypool.tile([P, 4, E], BF16, name="yraw")
            src = y[i, h * 512 : (h + 1) * 512, :].rearrange("(p t) e -> p t e", t=4)
            w = 4 // pieces
            for q in range(pieces):
                nc.sync.dma_start(out=yraw[:, q * w : (q + 1) * w, :], in_=src[:, q * w : (q + 1) * w, :])
            yraws[j] = yraw

        def load_x(j):
            i, h = divmod(j, 2)
            xraw = xpool.tile([P, 4, D], BF16, name="xraw")
            nc.sync.dma_start(out=xraw[:], in_=x[i, h * 512 : (h + 1) * 512, :].rearrange("(p t) d -> p t d", t=4))
            xraws[j] = xraw

        nc.vector.memset(wsc[:].bitcast(I32), 0)
        nc.vector.memset(warm[:], 0.0)
        nc.vector.memset(brow[:], 0.0)
        nc.vector.memset(ones[:], 1.0)
        nc.scalar.activation(warm[:], warm[:], ACT.Exp)
        make_identity(nc, ident[:])
        nc.gpsimd.memset(neghalf[:], -0.5)
        load_y(0, 2)
        nc.sync.dma_start(out=wt[:].bitcast(I32), in_=w_words.rearrange("g p n t -> p g (n t)").bitcast(I32))
        for q in range(4):
            nc.sync.dma_start(
                out=wsc[32 * q : 32 * q + 4, :].bitcast(I32).rearrange("p (g n) -> p g n", g=2),
                in_=w_scales[:, 4 * q : 4 * q + 4, :].rearrange("g q n -> q g n").bitcast(I32),
            )
        nc.gpsimd.dma_start(out=brow[0:1, :], in_=b.rearrange("(o k) -> o k", o=1))
        nc.gpsimd.dma_start(out=tb[:], in_=t.rearrange("(g p t) -> p g t", p=P, t=4))
        load_x(0)
        load_y(1)
        load_x(1)
        nc.sync.dma_start(out=cb[:], in_=c.rearrange("(a p) d -> p a d", p=P))
        load_y(2)
        load_x(2)
        load_y(3)
        load_x(3)
        nc.gpsimd.tensor_scalar(out=cneg[:], in0=cb[:], scalar1=-1.0, scalar2=0.0, op0=ALU.mult, op1=ALU.add)

        st8 = {}

        def gen_y(j):
            words = yraws[j][:].rearrange("p t e -> p (t e)").bitcast(F32)
            yg = work.tile([P, 2, 512, 4], BF16, align_bytes=64, name="yg")
            yg_w = yg[:].rearrange("p g n e -> p (g n e)").bitcast(F32)
            st8["yg", j] = yg
            banks = []
            for tp in range(2):
                for g in range(2):
                    banks.append((tp, g))
            return words, yg_w, banks

        def y_bank(j, n, words, yg_w, banks, engine):
            tp, g = banks[n]
            yt = yt_ps.tile([P, 2, 2, P], F32, name="yt")
            for u in range(2):
                for a in range(2):
                    base = (2 * tp + a) * 512 + 256 * g
                    nc.tensor.transpose(yt[:, u, a, :], words[:, base + u : base + 256 : 2], ident[:])
            engine(
                out=yg_w[:, g * 1024 + tp * 512 : g * 1024 + (tp + 1) * 512].rearrange("p (n u) -> p n u", u=2),
                in_=yt[:].rearrange("p u a n -> p (a n) u"),
            )

        def quant_y(j):
            yg = st8["yg", j]
            yc = work.tile([P, 2, 512], U32, align_bytes=64, name="yc")
            ys = work.tile([P, 2, 512], U8, align_bytes=64, name="ys")
            nc.vector.quantize_mx(
                out=yc[:].rearrange("p g n -> p (g n)").bitcast(FP8X4),
                scales=ys[:].rearrange("p g n -> p (g n)"),
                in_=yg[:].rearrange("p g n e -> p (g n e)"),
            )
            st8["yc", j] = (yc, ys)

        def logits(j):
            yc, ys = st8["yc", j]
            lgs = []
            for tp in range(2):
                lg = lg_ps.tile([P, 2, K], F32, name="lg")
                for a in range(2):
                    tt = 2 * tp + a
                    for g in range(2):
                        nc.tensor.matmul_mx(
                            out=lg[:, a, :],
                            lhsT=yc[:, g, tt * P : (tt + 1) * P].bitcast(FP8X4),
                            lhsT_scale=ys[:, g, tt * P : (tt + 1) * P],
                            rhs=wt[:, g, :].bitcast(FP8X4),
                            rhs_scale=wsc[:, g * K : (g + 1) * K],
                            start=(g == 0),
                            stop=(g == 1),
                        )
                lgs.append(lg)
            st8["lg", j] = lgs

        def add_max(j):
            zs = []
            for tp in range(2):
                z = three.tile([P, 2, K], F32, name="z")
                nc.vector.tensor_tensor(out=z[:], in0=st8["lg", j][tp][:], in1=bias[:], op=ALU.add)
                zs.append(z)
            nmx = work.tile([P, 4], F32, name="nmx")
            for tp in range(2):
                nc.vector.tensor_reduce(out=nmx[:, 2 * tp : 2 * tp + 2], in_=zs[tp][:], axis=AX.X, op=ALU.max, negate=True)
            i, h = divmod(j, 2)
            if h == 0:
                st8["e", i] = work.tile([P, 8, K], F32, name="e")
                st8["rinv", i] = work.tile([P, 8], F32, name="rinv")
                st8["st", i] = work.tile([P, 8], F32, name="st")
            ssum = work.tile([P, 4], F32, name="ssum")
            st8["sm", j] = (zs, nmx, ssum)

        def exps(j, tp):
            i, h = divmod(j, 2)
            zs, nmx, ssum = st8["sm", j]
            for a in range(2):
                tt = 2 * tp + a
                nc.scalar.activation(
                    st8["e", i][:, 4 * h + tt, :], zs[tp][:, a, :], ACT.Exp, bias=nmx[:, tt : tt + 1], accum_out=ssum[:, tt : tt + 1]
                )

        def recip(j):
            i, h = divmod(j, 2)
            nc.vector.reciprocal(out=st8["rinv", i][:, 4 * h : 4 * h + 4], in_=st8["sm", j][2][:])

        def st_mul(j):
            i, h = divmod(j, 2)
            cols = slice(4 * h, 4 * h + 4)
            nc.vector.tensor_tensor(out=st8["st", i][:, cols], in0=st8["rinv", i][:, cols], in1=tb[:, h, :], op=ALU.mult)

        def r_mul(j):
            i, h = divmod(j, 2)
            rg = work.tile([P, K, 4], BF16, align_bytes=64, name="rg")
            nc.vector.tensor_tensor(
                out=rg[:].rearrange("p (q k) t -> p q t k", k=4),
                in0=st8["e", i][:, 4 * h : 4 * h + 4, :].rearrange("p t (q k) -> p q t k", k=4),
                in1=st8["st", i][:, 4 * h : 4 * h + 4].unsqueeze(1).unsqueeze(3).to_broadcast([P, K // 4, 4, 4]),
                op=ALU.mult,
            )
            st8["rg", j] = rg

        def quant_r(j):
            rc = four.tile([P, K], U32, align_bytes=64, name="rc")
            rs = four.tile([P, K], U8, align_bytes=64, name="rs")
            nc.vector.quantize_mx(out=rc[:].bitcast(FP8X4), scales=rs[:], in_=st8["rg", j][:].rearrange("p k t -> p (k t)"))
            st8["rc", j] = (rc, rs)

        def x_vector(j):
            xg = work.tile([P, D, 4], BF16, align_bytes=64, name="xg")
            st8["xg", j] = xg
            dst = xg[:].rearrange("p (q i) t -> p q t i", i=4)
            src = xraws[j][:].rearrange("p t (q i) -> p q t i", i=4)
            nc.vector.tensor_copy(out=dst[:, : XV // 4], in_=src[:, : XV // 4])

        def x_scalar(j):
            dst = st8["xg", j][:].rearrange("p (q i) t -> p q t i", i=4)
            src = xraws[j][:].rearrange("p t (q i) -> p q t i", i=4)
            nc.scalar.copy(out=dst[:, XV // 4 :], in_=src[:, XV // 4 :])

        def quant_x(j):
            xc = six.tile([P, D], U32, align_bytes=64, name="xc")
            xs = six.tile([P, D], U8, align_bytes=64, name="xs")
            nc.vector.quantize_mx(out=xc[:].bitcast(FP8X4), scales=xs[:], in_=st8["xg", j][:].rearrange("p d t -> p (d t)"))
            st8["xc", j] = (xc, xs)

        def mass(j, kt):
            i, h = divmod(j, 2)
            if h == 0 and kt == 0:
                st8["m", i] = m_ps.tile([P, 4], F32, name="m")
                st8["msum", i] = work.tile([P, 2], F32, name="msum")
            m = st8["m", i]
            for tt in range(4):
                nc.tensor.matmul(
                    out=m[:, 2 * kt + h : 2 * kt + h + 1],
                    lhsT=st8["e", i][:, 4 * h + tt, kt * P : (kt + 1) * P],
                    rhs=st8["rinv", i][:, 4 * h + tt : 4 * h + tt + 1],
                    start=(tt == 0),
                    stop=(tt == 3),
                )

        def mass_sum(i, kt):
            nc.vector.tensor_reduce(
                out=st8["msum", i][:, kt : kt + 1], in_=st8["m", i][:, 2 * kt : 2 * kt + 2], axis=AX.X, op=ALU.add
            )

        def sums(i, kt, pool, name):
            tiles = []
            for dh in range(2):
                s = pool.tile([P, 512], F32, name=name)
                for h in range(2):
                    rc, rs = st8["rc", 2 * i + h]
                    xc, xs = st8["xc", 2 * i + h]
                    nc.tensor.matmul_mx(
                        out=s[:],
                        lhsT=rc[:, kt * P : (kt + 1) * P].bitcast(FP8X4),
                        lhsT_scale=rs[:, kt * P : (kt + 1) * P],
                        rhs=xc[:, dh * 512 : (dh + 1) * 512].bitcast(FP8X4),
                        rhs_scale=xs[:, dh * 512 : (dh + 1) * 512],
                        start=(h == 0),
                        stop=(h == 1),
                    )
                tiles.append(s)
            st8["s", i, kt] = tiles

        def centre(i, kt, dh):
            if dh == 0:
                st8["v", i, kt] = work.tile([P, D], F32, name="v")
            cols = slice(dh * 512, (dh + 1) * 512)
            nc.vector.scalar_tensor_tensor(
                out=st8["v", i, kt][:, cols],
                in0=cneg[:, kt, cols],
                scalar=st8["msum", i][:, kt : kt + 1],
                in1=st8["s", i, kt][dh][:],
                op0=ALU.mult,
                op1=ALU.add,
            )

        def square(i, kt):
            ss = three.tile([P, 1], F32, name="ss")
            nc.scalar.activation(sq[:], st8["v", i, kt][:], ACT.Square, accum_out=ss[:])
            ms = three.tile([P, 1], F32, name="ms")
            nc.gpsimd.tensor_scalar(out=ms[:], in0=ss[:], scalar1=1.0 / D, scalar2=EPS, op0=ALU.mult, op1=ALU.add)
            rstd = three.tile([P, 1], F32, name="rstd")
            nc.gpsimd.tensor_tensor(out=rstd[:], in0=ms[:], in1=neghalf[:], op=ALU.pow)
            st8["rstd", i, kt] = rstd

        def scale_out(i, kt, on_vector):
            of = work.tile([P, D], F32, name="of")
            if on_vector:
                nc.vector.tensor_scalar(
                    out=of[:], in0=st8["v", i, kt][:], scalar1=st8["rstd", i, kt][:], scalar2=None, op0=ALU.mult
                )
            else:
                nc.scalar.activation(of[:], st8["v", i, kt][:], ACT.Copy, scale=st8["rstd", i, kt][:])
            nc.sync.dma_start(out=out_0[i, kt * P : (kt + 1) * P, :], in_=of[:])
            st8["of", i, kt] = of

        def round_out(i, kt):
            ob = work.tile([P, D], BF16, name="ob")
            nc.vector.tensor_scalar(
                out=ob[:], in0=st8["v", i, kt][:], scalar1=st8["rstd", i, kt][:], scalar2=None, op0=ALU.mult
            )
            st8["ob", i, kt] = ob

        def turn_out(i, kt):
            words = st8["ob", i, kt][:].bitcast(F32)
            ot = yt_ps.tile([P, 2, 2, P], F32, name="yt")
            for g in range(2):
                for u in range(2):
                    nc.tensor.transpose(ot[:, g, u, :], words[:, 256 * g + u : 256 * (g + 1) : 2], ident[:])
            st8["ot", i, kt] = ot

        def copy_out(i, kt):
            if kt == 0:
                st8["pg", i] = work.tile([P, 2, K, 4], BF16, align_bytes=64, name="pg")
            pg_w = st8["pg", i][:].rearrange("p g k e -> p (g k e)").bitcast(F32).rearrange("p (g k u) -> p g k u", g=2, u=2)
            nc.scalar.copy(
                out=pg_w[:, :, kt * P : (kt + 1) * P, :],
                in_=st8["ot", i, kt][:].rearrange("p g u k -> p g k u"),
            )

        def quant_out(i):
            pc = work.tile([P, 2 * K], U32, align_bytes=64, name="pc")
            ps = work.tile([P, 2 * K], U8, align_bytes=64, name="ps")
            nc.vector.quantize_mx(
                out=pc[:].bitcast(FP8X4), scales=ps[:], in_=st8["pg", i][:].rearrange("p g k e -> p (g k e)")
            )
            rows = slice(i * K, (i + 1) * K)
            nc.sync.dma_start(
                out=out_1[:, :, rows, :].rearrange("g p k t -> p g (k t)").bitcast(I32),
                in_=pc[:].bitcast(I32).rearrange("p (g k) -> p g k", g=2),
            )
            for q in range(4):
                nc.sync.dma_start(
                    out=out_2[:, 4 * q : 4 * q + 4, rows].rearrange("g q k -> q g k").bitcast(I32),
                    in_=ps[32 * q : 32 * q + 4, :].bitcast(I32).rearrange("p (g k) -> p g k", g=2),
                )

        words, yg_w, banks = gen_y(0)
        for n in range(4):
            y_bank(0, n, words, yg_w, banks, nc.scalar.copy if n % 2 == 0 else nc.vector.tensor_copy)
        bps = lg_ps.tile([P, 2, K], F32, name="lg")
        for a in range(2):
            nc.tensor.matmul(out=bps[:, a, :], lhsT=ones[:], rhs=brow[:], start=True, stop=True)
        nc.vector.tensor_copy(out=bias[:], in_=bps[:])
        quant_y(0)
        logits(0)
        x_vector(0)
        x_scalar(0)

        for s in range(HALVES):
            nxt = s + 1 if s + 1 < HALVES else None
            ep = divmod(s - 2, 2) if s >= 2 else None
            old = divmod(s - 3, 2) if s >= 3 else None
            add_max(s)
            if nxt is not None:
                words, yg_w, banks = gen_y(nxt)
                y_bank(nxt, 0, words, yg_w, banks, nc.scalar.copy)
                y_bank(nxt, 1, words, yg_w, banks, nc.scalar.copy)
            if old:
                round_out(*old)
            exps(s, 0)
            if ep:
                sums(ep[0], ep[1], s_ps, "s")
            if nxt is not None:
                y_bank(nxt, 2, words, yg_w, banks, nc.scalar.copy)
                y_bank(nxt, 3, words, yg_w, banks, nc.scalar.copy)
                if 4 <= nxt + 3 < HALVES:
                    load_y(nxt + 3)
            if s >= 1:
                mass(s - 1, 1)
            if old:
                turn_out(*old)
            exps(s, 1)
            if old:
                copy_out(*old)
            quant_x(s)
            if ep:
                if ep[1] == 0:
                    mass_sum(ep[0], 0)
                centre(ep[0], ep[1], 0)
                centre(ep[0], ep[1], 1)
            if nxt is not None:
                x_vector(nxt)
                quant_y(nxt)
                logits(nxt)
            recip(s)
            if ep and ep[1] == 0:
                mass_sum(ep[0], 1)
            st_mul(s)
            mass(s, 0)
            if ep:
                square(*ep)
            if nxt is not None:
                x_scalar(nxt)
                if 4 <= nxt + 3 < HALVES:
                    load_x(nxt + 3)
            r_mul(s)
            if old and old[1] == 1:
                quant_out(old[0])
            quant_r(s)
            if ep:
                scale_out(ep[0], ep[1], False)

        sums(3, 0, s_ps, "s")
        mass(7, 1)
        sums(3, 1, lg_ps, "lg")
        round_out(2, 1)
        turn_out(2, 1)
        copy_out(2, 1)
        mass_sum(3, 0)
        centre(3, 0, 0)
        centre(3, 0, 1)
        square(3, 0)
        mass_sum(3, 1)
        centre(3, 1, 0)
        centre(3, 1, 1)
        square(3, 1)
        quant_out(2)
        round_out(3, 0)
        turn_out(3, 0)
        scale_out(3, 0, True)
        round_out(3, 1)
        turn_out(3, 1)
        copy_out(3, 0)
        copy_out(3, 1)
        scale_out(3, 1, False)
        quant_out(3)
